import numpy as np
import ml_dtypes


def mxq(x, axis, fmt="e4m3"):
    dtype, down = {"e4m3": (ml_dtypes.float8_e4m3fn, 7), "e5m2": (ml_dtypes.float8_e5m2, 14)}[fmt]
    v = np.moveaxis(np.asarray(x, np.float32).astype(ml_dtypes.bfloat16).astype(np.float64), axis, -1)
    blocks = v.reshape(v.shape[:-1] + (-1, 32))
    amax = np.abs(blocks).max(-1, keepdims=True)
    byte = np.maximum(np.where(amax > 0, np.frexp(amax)[1] - 1 + 127, 0) - down, 1)
    scale = np.exp2(byte - 127.0)
    codes = (blocks / scale).astype(np.float32).astype(dtype).astype(np.float64)
    return np.moveaxis((codes * scale).reshape(v.shape), -1, axis)


WIDE = False


def mx_kscale(k):
    if not WIDE:
        return np.ones(k)
    levels = np.array([10, -10, 5, -5, 0])
    if k % 512:
        return np.exp2(np.random.permutation(np.resize(levels, k // 32))).repeat(32)
    a = np.empty((k // 512, 16))
    for p in range(k // 512):
        a[p, :8] = np.random.permutation(np.resize(levels, 8))
        for g in range(8):
            far = levels[np.abs(levels - a[p, g]) >= 10]
            a[p, g + 8] = far[np.random.randint(len(far))]
    return np.exp2(a.ravel()).repeat(32)


BF16 = ml_dtypes.bfloat16


def bf(x):
    return np.asarray(x, np.float32).astype(BF16)


def f64(x):
    return np.asarray(x).astype(np.float64)


E2M1 = np.array([0.0, 0.5, 1.0, 1.5, 2.0, 3.0, 4.0, 6.0, -0.0, -0.5, -1.0, -1.5, -2.0, -3.0, -4.0, -6.0])


def pack_weight(w, fmt):
    k, n = w.shape
    w = f64(bf(w)).reshape(k // 32, 32, n)
    amax = np.abs(w).max(1)
    if fmt == "e4m3":
        byte = np.frexp(amax)[1] - 1 + 127 - 7
    else:
        mant, ex = np.frexp(amax / 6.0)
        byte = np.where(mant > 0.5, ex, ex - 1) + 127
    byte = np.clip(np.where(amax > 0, byte, 1), 1, 254)
    scaled = (w * np.exp2(127.0 - byte)[:, None, :]).reshape(k, n).astype(np.float32)
    by_word = np.ascontiguousarray(scaled.reshape(k // 512, 128, 4, n).transpose(0, 1, 3, 2))
    if fmt == "e4m3":
        words = by_word.astype(ml_dtypes.float8_e4m3fn).view(np.uint8)
    else:
        c = by_word.astype(ml_dtypes.float4_e2m1fn).view(np.uint8) & 0xF
        words = c[..., 0::2] | (c[..., 1::2] << 4)
    return np.ascontiguousarray(words), np.ascontiguousarray(byte.astype(np.uint8).reshape(k // 512, 16, n))


def unpack_weight(words, scales, fmt):
    g, p, n, _ = words.shape
    if fmt == "e4m3":
        vals = np.ascontiguousarray(words).view(ml_dtypes.float8_e4m3fn).astype(np.float64)
    else:
        nib = np.empty((g, p, n, 4), np.uint8)
        nib[..., 0::2] = words & 0xF
        nib[..., 1::2] = words >> 4
        vals = E2M1[nib]
    vals = vals * np.repeat(np.exp2(scales.astype(np.float64) - 127.0), 8, axis=1)[..., None]
    return vals.transpose(0, 1, 3, 2).reshape(g * 512, n)
def pack4(w):
    words, scales = pack_weight(w, "e2m1")
    return words.reshape(words.shape[0], 128, -1), scales


def unpack4(words, scales):
    return unpack_weight(words.reshape(words.shape[0], 128, -1, 2), scales, "e2m1")


N, K, L = 1024, 1024, 512


def setup_inputs():
    s, r, t = mx_kscale(K), mx_kscale(L), mx_kscale(N)
    u = np.random.standard_normal((K, N)) / np.sqrt(K) * s[:, None] / t
    v = np.random.standard_normal((K, N)) * N ** -0.25 / s[:, None] * t
    x = np.random.standard_normal((N, L)) * N ** -0.25 * r / t[:, None]
    w = np.random.standard_normal((L, N)) / np.sqrt(L) / r[:, None] * t
    d = 2.0 ** np.random.uniform(-1, 1, N)
    u_words, u_scales = pack4(u)
    v_words, v_scales = pack4(v)
    return {"u_words": u_words, "u_scales": u_scales,
            "v_words": v_words, "v_scales": v_scales,
            "x": bf(x), "w": bf(w),
            "left": bf(d * t), "right": bf(1 / (d * t))}


def reference(u_words, u_scales, v_words, v_scales, x, w, left, right):
    a = unpack4(u_words, u_scales).T @ unpack4(v_words, v_scales)
    b = mxq(f64(x), 1, "e4m3") @ mxq(f64(w), 0, "e4m3")
    ab = mxq(a, 1, "e4m3") @ mxq(b, 0, "e4m3")
    ba = mxq(b, 1, "e4m3") @ mxq(a, 0, "e4m3")
    return (ab - ba) * f64(left)[:, None] * f64(right)

@@ -1,0 +1,343 @@
+from contextlib import ExitStack
+
+import concourse.mybir as mybir
+from concourse.masks import make_identity
+
+N, K, L = 1024, 1024, 512
+FLOPS = 2 * N * N * K + 2 * N * N * L + 4 * N * N * N
+
+F32 = mybir.dt.float32
+BF16 = mybir.dt.bfloat16
+I32 = mybir.dt.int32
+U32 = mybir.dt.uint32
+U8 = mybir.dt.uint8
+FP8X4 = mybir.dt.float8_e4m3fn_x4
+FP4X4 = mybir.dt.float4_e2m1fn_x4
+MULT = mybir.AluOpType.mult
+
+P = 128
+H = 512
+
+
+def tile_diagonally_scaled_matrix_commutator_s12_kernel(
+    tc, u_words, u_scales, v_words, v_scales, x, w, left, right, out
+):
+    nc = tc.nc
+    with ExitStack() as ctx:
+        keep = ctx.enter_context(tc.tile_pool(name="keep", bufs=1))
+        work = ctx.enter_context(tc.tile_pool(name="work", bufs=3))
+        psum = ctx.enter_context(tc.psum_pool(name="psum", bufs=1))
+        ctx.enter_context(tc.manual_schedule())
+
+        def kept(name, width, dtype):
+            return keep.tile([P, width], dtype, name=name, align_bytes=64)
+
+        ring = {"banks": list(range(8)), "next": 0, "acc": 4}
+
+        def bank_tile(name, b):
+            return psum.tile([P, H], F32, name=name, tag="bank%d" % b)
+
+        def stage_bank(name):
+            b = ring["banks"][ring["next"] % len(ring["banks"])]
+            ring["next"] = ring["next"] + 1
+            return bank_tile(name, b)
+
+        def narrow_ring():
+            ring["banks"] = list(range(4))
+
+        def acc_bank(name):
+            b = ring["acc"]
+            ring["acc"] = 4 + (b + 1) % 4
+            return bank_tile(name, b)
+
+        u_plane = kept("u_plane", 2 * N, U8)
+        v_plane = kept("v_plane", 2 * N, U8)
+        u_sc = kept("u_sc", 2 * N, U8)
+        nc.vector.memset(v_plane[:].bitcast(I32), 0)
+        nc.vector.memset(u_sc[:].bitcast(I32), 0)
+        ident = kept("ident", P, F32)
+        make_identity(nc, ident[:])
+        left_rows = kept("left_rows", P, BF16)
+        nc.gpsimd.memset(left_rows[:], 0.0)
+
+        u_raw, v_codes, x_raw, w_raw = {}, {}, {}, {}
+
+        def load_words(store, name, words, h):
+            store[h] = kept("%s%d" % (name, h), 4 * H, U8)
+            nc.sync.dma_start(
+                out=store[h][:].bitcast(I32).rearrange("p (g c) -> p g c", g=2),
+                in_=words.bitcast(I32)[:, :, h * 256 : (h + 1) * 256].rearrange("g p c -> p g c"),
+            )
+
+        def load_plane(plane, scales):
+            for quad in range(4):
+                nc.sync.dma_start(
+                    out=plane[32 * quad : 32 * quad + 4, :].bitcast(I32).rearrange("r (g c) -> r g c", g=2),
+                    in_=scales.bitcast(I32)[:, 4 * quad : 4 * quad + 4, :].rearrange("g r c -> r g c"),
+                )
+
+        def load_x(h):
+            x_raw[h] = kept("x_raw%d" % h, 4 * L, BF16)
+            nc.sync.dma_start(
+                out=x_raw[h][:].rearrange("p (c k) -> p c k", c=4),
+                in_=x[h * H : (h + 1) * H, :].rearrange("(c p) k -> p c k", p=P),
+            )
+
+        def load_w(g):
+            w_raw[g] = kept("w_raw%d" % g, 4 * H, BF16)
+            nc.sync.dma_start(
+                out=w_raw[g][:].rearrange("p (j n) -> p j n", j=4),
+                in_=w[:, g * H : (g + 1) * H].rearrange("(p j) n -> p j n", j=4),
+            )
+
+        load_plane(u_plane, u_scales)
+        load_words(u_raw, "u_raw", u_words, 0)
+        load_words(v_codes, "v_codes", v_words, 0)
+        load_plane(v_plane, v_scales)
+        load_w(0)
+        load_x(0)
+        load_w(1)
+        load_words(v_codes, "v_codes", v_words, 1)
+        load_x(1)
+        load_words(u_raw, "u_raw", u_words, 1)
+        nc.sync.dma_start(out=left_rows[0:8, :], in_=left.rearrange("(c p) -> c p", p=P))
+        right_all = kept("right_all", N, BF16)
+        nc.sync.dma_start(out=right_all[:], in_=right.partition_broadcast(P))
+
+        u_codes = {}
+
+        def permute_u_scales():
+            for quad in range(4):
+                rows = slice(32 * quad, 32 * quad + 4)
+                nc.vector.tensor_copy(
+                    out=u_sc[rows, :].bitcast(I32).rearrange("p (s t q c) -> p s t q c", s=4, t=4, q=16),
+                    in_=u_plane[rows, :].bitcast(I32).rearrange("p (s q t c) -> p s t q c", s=4, t=4, q=16),
+                )
+
+        def permute_u(g):
+            u_codes[g] = kept("u_codes%d" % g, 4 * H, U8)
+            nc.vector.tensor_copy(
+                out=u_codes[g][:].bitcast(I32).rearrange("p (s t q c) -> p s t q c", s=2, t=4, q=16),
+                in_=u_raw[g][:].bitcast(I32).rearrange("p (s q t c) -> p s t q c", s=2, t=4, q=16),
+            )
+
+        grouped, quant = {}, {}
+
+        def new_grouped(key):
+            grouped[key] = work.tile([P, 4 * H], BF16, name="grouped_%s" % (key,), tag="grouped", bufs=8, align_bytes=64)
+            return grouped[key]
+
+        def quantize(key):
+            codes = kept("codes_%s" % (key,), H, U32)
+            scales = kept("scales_%s" % (key,), H, U8)
+            nc.vector.quantize_mx(out=codes[:].bitcast(FP8X4), scales=scales[:], in_=grouped[key][:])
+            quant[key] = (codes, scales)
+
+        def turn_x(h, new_bank=stage_bank, copy=nc.scalar.copy):
+            dst = new_grouped("x%d" % h)[:].bitcast(F32).rearrange("p (u a q s e) -> p a u q s e", u=2, a=2, q=8, e=2)
+            words = x_raw[h][:].bitcast(F32)
+            banks = []
+            for a in range(2):
+                bank = new_bank("xt%d%d" % (h, a))
+                banks.append(bank)
+                for e in range(2):
+                    for c in range(2):
+                        c0 = (2 * a + c) * 256
+                        nc.tensor.transpose(bank[:, (2 * e + c) * P : (2 * e + c + 1) * P], words[:, c0 + e : c0 + 256 : 2], ident[:])
+            for a in range(2):
+                copy(out=dst[:, a], in_=banks[a][:].rearrange("p (e q u s) -> p u q s e", e=2, q=8, u=2))
+
+        def group_w(g):
+            dst = new_grouped("w%d" % g)
+            nc.vector.tensor_copy(
+                out=dst[:].rearrange("p (t q r j) -> p t q r j", t=4, q=16, j=4),
+                in_=w_raw[g][:].rearrange("p (j q t r) -> p t q r j", j=4, q=16, t=4),
+            )
+
+        plain = {}
+
+        def product(kind, g, h, t):
+            key = "%s%d%d" % (kind, g, h)
+            if t == 0:
+                plain[key] = work.tile([P, 4 * H], BF16, name="plain_" + key, tag="plain", bufs=4, align_bytes=64)
+            bank = stage_bank("mm_%s%d" % (key, t))
+            dst = plain[key][:, t * H : (t + 1) * H]
+            if kind == "a":
+                for s in range(2):
+                    nc.tensor.matmul_mx(
+                        out=bank[:],
+                        lhsT=u_codes[g][:, s * 1024 + t * 256 : s * 1024 + (t + 1) * 256].bitcast(FP4X4),
+                        lhsT_scale=u_sc[:, s * N + g * H + t * P : s * N + g * H + (t + 1) * P],
+                        rhs=v_codes[h][:, s * 1024 : (s + 1) * 1024].bitcast(FP4X4),
+                        rhs_scale=v_plane[:, s * N + h * H : s * N + (h + 1) * H],
+                        start=(s == 0),
+                        stop=(s == 1),
+                    )
+                nc.scalar.copy(
+                    out=dst.rearrange("p (u q s) -> p u q s", u=2, q=16),
+                    in_=bank[:].rearrange("p (q u s) -> p u q s", u=2, q=16),
+                )
+            else:
+                wc, ws = quant["w%d" % g]
+                xc, xs = quant["x%d" % h]
+                nc.tensor.matmul_mx(
+                    out=bank[:],
+                    lhsT=wc[:, t * P : (t + 1) * P].bitcast(FP8X4),
+                    lhsT_scale=ws[:, t * P : (t + 1) * P],
+                    rhs=xc[:].bitcast(FP8X4),
+                    rhs_scale=xs[:],
+                    start=True,
+                    stop=True,
+                )
+                nc.scalar.copy(out=dst, in_=bank[:])
+
+        def weave(key):
+            dst = new_grouped("s" + key)[:].rearrange("p (q u s t) -> p u q s t", q=16, u=2, t=4)
+            src = plain[key][:].rearrange("p (t u q s) -> p u q s t", t=4, u=2, q=16)
+            if key[0] == "a":
+                nc.vector.tensor_copy(out=dst.rearrange("p u q s t -> p q u s t"), in_=src.rearrange("p u q s t -> p q u s t"))
+            else:
+                for u in range(2):
+                    nc.vector.tensor_scalar(out=dst[:, u], in0=src[:, u], scalar1=-1.0, scalar2=None, op0=MULT)
+
+        def turn(key, new_bank=stage_bank, copy=nc.scalar.copy):
+            dst = new_grouped("t" + key)[:].bitcast(F32).rearrange("p (q a t r u) -> p a q t r u", q=16, a=2, t=2, u=2)
+            words = plain[key][:].bitcast(F32)
+            banks = []
+            for a in range(2):
+                bank = new_bank("tr_%s%d" % (key, a))
+                banks.append(bank)
+                for j in range(4):
+                    nc.tensor.transpose(bank[:, j * P : (j + 1) * P], words[:, (4 * a + j) * P : (4 * a + j + 1) * P], ident[:])
+            for a in range(2):
+                copy(out=dst[:, a], in_=banks[a][:].rearrange("p (t u q r) -> p q t r u", t=2, u=2, q=16))
+
+        left_cols = kept("left_cols", 8, F32)
+
+        def turn_left():
+            rows32 = kept("left_rows32", P, F32)
+            nc.gpsimd.tensor_copy(out=rows32[:], in_=left_rows[:])
+            bank = stage_bank("left_bank")
+            nc.tensor.transpose(bank[:, 0:P], rows32[:], ident[:])
+            nc.scalar.copy(out=left_cols[:], in_=bank[:, 0:8])
+
+        def operands(a, b, term):
+            k = term % 2
+            if term < 2:
+                return quant["ta%d%d" % (a, k)], quant["tb%d%d" % (b, k)]
+            return quant["sb%d%d" % (k, a)], quant["sa%d%d" % (k, b)]
+
+        acc, done = {}, {}
+
+        def accumulate(a, b, c, term, new_bank=acc_bank):
+            key = (a, b, c)
+            if key not in acc:
+                acc[key] = new_bank("acc%d%d%d" % key)
+                done[key] = 0
+            (lc, ls), (rc, rs) = operands(a, b, term)
+            nc.tensor.matmul_mx(
+                out=acc[key][:],
+                lhsT=lc[:, c * P : (c + 1) * P].bitcast(FP8X4),
+                lhsT_scale=ls[:, c * P : (c + 1) * P],
+                rhs=rc[:].bitcast(FP8X4),
+                rhs_scale=rs[:],
+                start=(done[key] == 0),
+                stop=(done[key] == 3),
+            )
+            done[key] = done[key] + 1
+
+        def finish(a, b, c):
+            key = (a, b, c)
+            res = work.tile([P, H], F32, name="res%d%d%d" % key, tag="res", bufs=6)
+            i = 4 * a + c
+            nc.vector.scalar_tensor_tensor(
+                out=res[:], in0=acc[key][:], scalar=left_cols[:, i : i + 1],
+                in1=right_all[:, b * H : (b + 1) * H], op0=MULT, op1=MULT,
+            )
+            nc.sync.dma_start(out=out[i * P : (i + 1) * P, b * H : (b + 1) * H], in_=res[:])
+
+        def run(jobs):
+            for job in jobs:
+                accumulate(*job)
+
+        def products(key, fill=()):
+            fill = list(fill)
+            for t in range(4):
+                product(key[0], int(key[1]), int(key[2]), t)
+                for job in fill[t::4]:
+                    if job:
+                        accumulate(*job)
+
+        def terms(a, b, term):
+            return [(a, b, c, term) for c in range(4)]
+
+        VC = nc.vector.tensor_copy
+        permute_u_scales()
+        permute_u(0)
+        products("a00")
+        group_w(0)
+        turn_x(0)
+        quantize("w0")
+        group_w(1)
+        weave("a00")
+        quantize("x0")
+        products("a01")
+        permute_u(1)
+        quantize("sa00")
+        turn("a00")
+        products("b00")
+        weave("a01")
+        quantize("ta00")
+        turn_x(1, copy=VC)
+        turn("a01")
+        quantize("sa01")
+        quantize("x1")
+        weave("b00")
+        products("a10")
+        quantize("w1")
+        quantize("sb00")
+        narrow_ring()
+        turn("b00")
+        products("b01", [None, None] + terms(0, 0, 2)[:2])
+        quantize("ta01")
+        weave("a10")
+        quantize("tb00")
+        quantize("sa10")
+        turn("a10")
+        products("b10", terms(0, 0, 2)[2:] + terms(0, 0, 0)[:2])
+        weave("b01")
+        quantize("ta10")
+        quantize("sb01")
+        turn("b01")
+        turn_left()
+        products("a11", terms(0, 0, 0)[2:])
+        weave("b10")
+        quantize("tb01")
+        quantize("sb10")
+        turn("b10")
+        products("b11", terms(0, 0, 1) + terms(0, 0, 3))
+        weave("a11")
+        finish(0, 0, 0)
+        finish(0, 0, 1)
+        quantize("sa11")
+        finish(0, 0, 2)
+        finish(0, 0, 3)
+        quantize("tb10")
+        turn("a11")
+        weave("b11")
+        run(terms(0, 1, 2))
+        turn("b11")
+        quantize("ta11")
+        quantize("sb11")
+        run(terms(0, 1, 0) + terms(0, 1, 3))
+        quantize("tb11")
+        for c in range(4):
+            for term in (0, 2, 1, 3):
+                accumulate(1, 0, c, term, stage_bank)
+            finish(1, 0, c)
+            accumulate(0, 1, c, 1)
+            finish(0, 1, c)
+        for c in range(4):
+            for term in range(4):
+                accumulate(1, 1, c, term)
+            finish(1, 1, c)

@@ -17,6 +17,7 @@ MULT = mybir.AluOpType.mult
 
 P = 128
 H = 512
+WARM = 20
 
 
 def tile_diagonally_scaled_matrix_commutator_s12_kernel(
@@ -50,11 +51,22 @@ def tile_diagonally_scaled_matrix_commutator_s12_kernel(
             ring["acc"] = 4 + (b + 1) % 4
             return bank_tile(name, b)
 
+        warm_in = kept("warm_in", 4 * P, BF16)
+        warm_codes = kept("warm_codes", P, U32)
+        warm_scales = kept("warm_scales", P, U8)
+        nc.vector.memset(warm_in[:], 0.0)
         u_plane = kept("u_plane", 2 * N, U8)
         v_plane = kept("v_plane", 2 * N, U8)
         u_sc = kept("u_sc", 2 * N, U8)
         nc.vector.memset(v_plane[:].bitcast(I32), 0)
+        nc.vector.quantize_mx(out=warm_codes[:].bitcast(FP8X4), scales=warm_scales[:], in_=warm_in[:])
         nc.vector.memset(u_sc[:].bitcast(I32), 0)
+        warm_bank = bank_tile("warm_bank", 7)
+        for rep in range(WARM):
+            nc.tensor.matmul_mx(
+                out=warm_bank[:, 0:P], lhsT=warm_codes[:].bitcast(FP8X4), lhsT_scale=warm_scales[:],
+                rhs=warm_codes[:].bitcast(FP8X4), rhs_scale=warm_scales[:], start=True, stop=True,
+            )
         ident = kept("ident", P, F32)
         make_identity(nc, ident[:])
         left_rows = kept("left_rows", P, BF16)
@@ -69,9 +81,9 @@ def tile_diagonally_scaled_matrix_commutator_s12_kernel(
                 in_=words.bitcast(I32)[:, :, h * 256 : (h + 1) * 256].rearrange("g p c -> p g c"),
             )
 
-        def load_plane(plane, scales):
+        def load_plane(plane, scales, queues):
             for quad in range(4):
-                nc.sync.dma_start(
+                queues[quad].dma_start(
                     out=plane[32 * quad : 32 * quad + 4, :].bitcast(I32).rearrange("r (g c) -> r g c", g=2),
                     in_=scales.bitcast(I32)[:, 4 * quad : 4 * quad + 4, :].rearrange("g r c -> r g c"),
                 )
@@ -90,16 +102,16 @@ def tile_diagonally_scaled_matrix_commutator_s12_kernel(
                 in_=w[:, g * H : (g + 1) * H].rearrange("(p j) n -> p j n", j=4),
             )
 
-        load_plane(u_plane, u_scales)
+        load_plane(u_plane, u_scales, [nc.sync] * 4)
+        load_x(0)
         load_words(u_raw, "u_raw", u_words, 0)
         load_words(v_codes, "v_codes", v_words, 0)
-        load_plane(v_plane, v_scales)
+        load_plane(v_plane, v_scales, [nc.sync] + [nc.scalar] * 3)
         load_w(0)
-        load_x(0)
-        load_w(1)
         load_words(v_codes, "v_codes", v_words, 1)
-        load_x(1)
         load_words(u_raw, "u_raw", u_words, 1)
+        load_x(1)
+        load_w(1)
         nc.sync.dma_start(out=left_rows[0:8, :], in_=left.rearrange("(c p) -> c p", p=P))
         right_all = kept("right_all", N, BF16)
         nc.sync.dma_start(out=right_all[:], in_=right.partition_broadcast(P))
@@ -159,7 +171,7 @@ def tile_diagonally_scaled_matrix_commutator_s12_kernel(
         def product(kind, g, h, t):
             key = "%s%d%d" % (kind, g, h)
             if t == 0:
-                plain[key] = work.tile([P, 4 * H], BF16, name="plain_" + key, tag="plain", bufs=4, align_bytes=64)
+                plain[key] = work.tile([P, 4 * H], BF16, name="plain_" + key, tag="plain", bufs=5, align_bytes=64)
             bank = stage_bank("mm_%s%d" % (key, t))
             dst = plain[key][:, t * H : (t + 1) * H]
             if kind == "a":
@@ -214,9 +226,12 @@ def tile_diagonally_scaled_matrix_commutator_s12_kernel(
 
         left_cols = kept("left_cols", 8, F32)
 
+        rows32 = kept("left_rows32", P, F32)
+
+        def widen_left():
+            nc.vector.tensor_copy(out=rows32[:], in_=left_rows[:])
+
         def turn_left():
-            rows32 = kept("left_rows32", P, F32)
-            nc.gpsimd.tensor_copy(out=rows32[:], in_=left_rows[:])
             bank = stage_bank("left_bank")
             nc.tensor.transpose(bank[:, 0:P], rows32[:], ident[:])
             nc.scalar.copy(out=left_cols[:], in_=bank[:, 0:8])
@@ -256,6 +271,30 @@ def tile_diagonally_scaled_matrix_commutator_s12_kernel(
             )
             nc.sync.dma_start(out=out[i * P : (i + 1) * P, b * H : (b + 1) * H], in_=res[:])
 
+        def last_tile(a, b, c):
+            i = 4 * a + c
+            for half in range(2):
+                cols = slice(half * 256, (half + 1) * 256)
+                bank = acc_bank("last%d" % half)
+                for term in range(4):
+                    (lc, ls), (rc, rs) = operands(a, b, term)
+                    nc.tensor.matmul_mx(
+                        out=bank[:, 0:256],
+                        lhsT=lc[:, c * P : (c + 1) * P].bitcast(FP8X4),
+                        lhsT_scale=ls[:, c * P : (c + 1) * P],
+                        rhs=rc[:, cols].bitcast(FP8X4),
+                        rhs_scale=rs[:, cols],
+                        start=(term == 0),
+                        stop=(term == 3),
+                    )
+                res = work.tile([P, 256], F32, name="last_res%d" % half, tag="res", bufs=6)
+                out_cols = slice(b * H + half * 256, b * H + (half + 1) * 256)
+                nc.vector.scalar_tensor_tensor(
+                    out=res[:], in0=bank[:, 0:256], scalar=left_cols[:, i : i + 1],
+                    in1=right_all[:, out_cols], op0=MULT, op1=MULT,
+                )
+                nc.sync.dma_start(out=out[i * P : (i + 1) * P, out_cols], in_=res[:])
+
         def run(jobs):
             for job in jobs:
                 accumulate(*job)
@@ -274,43 +313,44 @@ def tile_diagonally_scaled_matrix_commutator_s12_kernel(
         VC = nc.vector.tensor_copy
         permute_u_scales()
         permute_u(0)
+        turn_x(0)
         products("a00")
         group_w(0)
-        turn_x(0)
-        quantize("w0")
-        group_w(1)
-        weave("a00")
         quantize("x0")
+        quantize("w0")
         products("a01")
+        weave("a00")
+        widen_left()
         permute_u(1)
-        quantize("sa00")
-        turn("a00")
         products("b00")
+        quantize("sa00")
         weave("a01")
-        quantize("ta00")
+        turn("a00")
         turn_x(1, copy=VC)
-        turn("a01")
-        quantize("sa01")
-        quantize("x1")
+        turn_left()
         weave("b00")
-        products("a10")
-        quantize("w1")
+        quantize("x1")
         quantize("sb00")
+        products("a10")
+        quantize("ta00")
+        group_w(1)
         narrow_ring()
         turn("b00")
-        products("b01", [None, None] + terms(0, 0, 2)[:2])
-        quantize("ta01")
-        weave("a10")
+        turn("a01")
+        quantize("sa01")
+        quantize("w1")
         quantize("tb00")
+        products("b01", terms(0, 0, 2))
+        weave("a10")
+        quantize("ta01")
         quantize("sa10")
         turn("a10")
-        products("b10", terms(0, 0, 2)[2:] + terms(0, 0, 0)[:2])
+        products("b10", terms(0, 0, 0))
         weave("b01")
         quantize("ta10")
         quantize("sb01")
         turn("b01")
-        turn_left()
-        products("a11", terms(0, 0, 0)[2:])
+        products("a11")
         weave("b10")
         quantize("tb01")
         quantize("sb10")
@@ -337,7 +377,8 @@ def tile_diagonally_scaled_matrix_commutator_s12_kernel(
             finish(1, 0, c)
             accumulate(0, 1, c, 1)
             finish(0, 1, c)
-        for c in range(4):
+        for c in range(3):
             for term in range(4):
                 accumulate(1, 1, c, term)
             finish(1, 1, c)
+        last_tile(1, 1, 3)

@@ -17,7 +17,7 @@ MULT = mybir.AluOpType.mult
 
 P = 128
 H = 512
-WARM = 20
+WARM = 24
 
 
 def tile_diagonally_scaled_matrix_commutator_s12_kernel(
@@ -103,16 +103,16 @@ def tile_diagonally_scaled_matrix_commutator_s12_kernel(
             )
 
         load_plane(u_plane, u_scales, [nc.sync] * 4)
-        load_x(0)
         load_words(u_raw, "u_raw", u_words, 0)
         load_words(v_codes, "v_codes", v_words, 0)
-        load_plane(v_plane, v_scales, [nc.sync] + [nc.scalar] * 3)
+        load_plane(v_plane, v_scales, [nc.sync] * 4)
+        load_x(0)
         load_w(0)
         load_words(v_codes, "v_codes", v_words, 1)
+        nc.sync.dma_start(out=left_rows[0:8, :], in_=left.rearrange("(c p) -> c p", p=P))
         load_words(u_raw, "u_raw", u_words, 1)
         load_x(1)
         load_w(1)
-        nc.sync.dma_start(out=left_rows[0:8, :], in_=left.rearrange("(c p) -> c p", p=P))
         right_all = kept("right_all", N, BF16)
         nc.sync.dma_start(out=right_all[:], in_=right.partition_broadcast(P))
 
@@ -161,17 +161,18 @@ def tile_diagonally_scaled_matrix_commutator_s12_kernel(
 
         def group_w(g):
             dst = new_grouped("w%d" % g)
-            nc.vector.tensor_copy(
-                out=dst[:].rearrange("p (t q r j) -> p t q r j", t=4, q=16, j=4),
-                in_=w_raw[g][:].rearrange("p (j q t r) -> p t q r j", j=4, q=16, t=4),
-            )
+            for c in range(2):
+                nc.vector.tensor_copy(
+                    out=dst[:].rearrange("p (t q c i j) -> p c t q j i", t=4, q=16, i=4, j=4)[:, c],
+                    in_=w_raw[g][:].rearrange("p (j q t c i) -> p c t q j i", j=4, q=16, t=4, i=4)[:, c],
+                )
 
         plain = {}
 
         def product(kind, g, h, t):
             key = "%s%d%d" % (kind, g, h)
             if t == 0:
-                plain[key] = work.tile([P, 4 * H], BF16, name="plain_" + key, tag="plain", bufs=5, align_bytes=64)
+                plain[key] = work.tile([P, 4 * H], BF16, name="plain_" + key, tag="plain", bufs=6, align_bytes=64)
             bank = stage_bank("mm_%s%d" % (key, t))
             dst = plain[key][:, t * H : (t + 1) * H]
             if kind == "a":
@@ -204,16 +205,24 @@ def tile_diagonally_scaled_matrix_commutator_s12_kernel(
                 nc.scalar.copy(out=dst, in_=bank[:])
 
         def weave(key):
-            dst = new_grouped("s" + key)[:].rearrange("p (q u s t) -> p u q s t", q=16, u=2, t=4)
-            src = plain[key][:].rearrange("p (t u q s) -> p u q s t", t=4, u=2, q=16)
+            dst = new_grouped("s" + key)
             if key[0] == "a":
-                nc.vector.tensor_copy(out=dst.rearrange("p u q s t -> p q u s t"), in_=src.rearrange("p u q s t -> p q u s t"))
+                nc.vector.tensor_scalar(
+                    out=dst[:].rearrange("p (c i t) -> p c t i", i=4, t=4),
+                    in0=plain[key][:].rearrange("p (t c i) -> p c t i", i=4, t=4),
+                    scalar1=-1.0, scalar2=None, op0=MULT,
+                )
             else:
                 for u in range(2):
-                    nc.vector.tensor_scalar(out=dst[:, u], in0=src[:, u], scalar1=-1.0, scalar2=None, op0=MULT)
+                    nc.vector.tensor_copy(
+                        out=dst[:].rearrange("p (q u c i t) -> p u q c t i", q=16, u=2, i=4, t=4)[:, u],
+                        in_=plain[key][:].rearrange("p (t u q c i) -> p u q c t i", q=16, u=2, i=4, t=4)[:, u],
+                    )
 
-        def turn(key, new_bank=stage_bank, copy=nc.scalar.copy):
-            dst = new_grouped("t" + key)[:].bitcast(F32).rearrange("p (q a t r u) -> p a q t r u", q=16, a=2, t=2, u=2)
+        def turn(key, new_bank=stage_bank, copy=(nc.scalar.copy, nc.scalar.copy)):
+            dst = new_grouped("t" + key)[:].bitcast(F32).rearrange(
+                "p (q a t r u) -> p a q t r u" if key[0] == "a" else "p (a q t r u) -> p a q t r u", q=16, a=2, t=2, u=2
+            )
             words = plain[key][:].bitcast(F32)
             banks = []
             for a in range(2):
@@ -222,7 +231,7 @@ def tile_diagonally_scaled_matrix_commutator_s12_kernel(
                 for j in range(4):
                     nc.tensor.transpose(bank[:, j * P : (j + 1) * P], words[:, (4 * a + j) * P : (4 * a + j + 1) * P], ident[:])
             for a in range(2):
-                copy(out=dst[:, a], in_=banks[a][:].rearrange("p (t u q r) -> p q t r u", t=2, u=2, q=16))
+                copy[a](out=dst[:, a], in_=banks[a][:].rearrange("p (t u q r) -> p q t r u", t=2, u=2, q=16))
 
         left_cols = kept("left_cols", 8, F32)
 
@@ -265,47 +274,55 @@ def tile_diagonally_scaled_matrix_commutator_s12_kernel(
             key = (a, b, c)
             res = work.tile([P, H], F32, name="res%d%d%d" % key, tag="res", bufs=6)
             i = 4 * a + c
-            nc.vector.scalar_tensor_tensor(
-                out=res[:], in0=acc[key][:], scalar=left_cols[:, i : i + 1],
-                in1=right_all[:, b * H : (b + 1) * H], op0=MULT, op1=MULT,
-            )
+            for u in range(2):
+                nc.vector.scalar_tensor_tensor(
+                    out=res[:].rearrange("p (q u s) -> p u q s", q=16, u=2)[:, u],
+                    in0=acc[key][:, u * 256 : (u + 1) * 256].rearrange("p (q s) -> p q s", q=16),
+                    scalar=left_cols[:, i : i + 1],
+                    in1=right_all[:, b * H : (b + 1) * H].rearrange("p (q u s) -> p u q s", q=16, u=2)[:, u],
+                    op0=MULT, op1=MULT,
+                )
             nc.sync.dma_start(out=out[i * P : (i + 1) * P, b * H : (b + 1) * H], in_=res[:])
 
         def last_tile(a, b, c):
             i = 4 * a + c
             for half in range(2):
-                cols = slice(half * 256, (half + 1) * 256)
-                bank = acc_bank("last%d" % half)
-                for term in range(4):
-                    (lc, ls), (rc, rs) = operands(a, b, term)
-                    nc.tensor.matmul_mx(
-                        out=bank[:, 0:256],
-                        lhsT=lc[:, c * P : (c + 1) * P].bitcast(FP8X4),
-                        lhsT_scale=ls[:, c * P : (c + 1) * P],
-                        rhs=rc[:, cols].bitcast(FP8X4),
-                        rhs_scale=rs[:, cols],
-                        start=(term == 0),
-                        stop=(term == 3),
-                    )
                 res = work.tile([P, 256], F32, name="last_res%d" % half, tag="res", bufs=6)
                 out_cols = slice(b * H + half * 256, b * H + (half + 1) * 256)
-                nc.vector.scalar_tensor_tensor(
-                    out=res[:], in0=bank[:, 0:256], scalar=left_cols[:, i : i + 1],
-                    in1=right_all[:, out_cols], op0=MULT, op1=MULT,
-                )
+                for u in range(2):
+                    cols = slice(u * 256 + half * P, u * 256 + (half + 1) * P)
+                    bank = stage_bank("last%d%d" % (half, u))
+                    for term in range(4):
+                        (lc, ls), (rc, rs) = operands(a, b, term)
+                        nc.tensor.matmul_mx(
+                            out=bank[:, 0:P],
+                            lhsT=lc[:, c * P : (c + 1) * P].bitcast(FP8X4),
+                            lhsT_scale=ls[:, c * P : (c + 1) * P],
+                            rhs=rc[:, cols].bitcast(FP8X4),
+                            rhs_scale=rs[:, cols],
+                            start=(term == 0),
+                            stop=(term == 3),
+                        )
+                    nc.vector.scalar_tensor_tensor(
+                        out=res[:].rearrange("p (q u s) -> p u q s", q=8, u=2)[:, u],
+                        in0=bank[:, 0:P].rearrange("p (q s) -> p q s", q=8),
+                        scalar=left_cols[:, i : i + 1],
+                        in1=right_all[:, out_cols].rearrange("p (q u s) -> p u q s", q=8, u=2)[:, u],
+                        op0=MULT, op1=MULT,
+                    )
                 nc.sync.dma_start(out=out[i * P : (i + 1) * P, out_cols], in_=res[:])
 
         def run(jobs):
             for job in jobs:
                 accumulate(*job)
 
-        def products(key, fill=()):
+        def products(key, fill=(), slots=range(4)):
             fill = list(fill)
-            for t in range(4):
-                product(key[0], int(key[1]), int(key[2]), t)
+            for t in slots:
                 for job in fill[t::4]:
                     if job:
                         accumulate(*job)
+                product(key[0], int(key[1]), int(key[2]), t)
 
         def terms(a, b, term):
             return [(a, b, c, term) for c in range(4)]
@@ -313,12 +330,12 @@ def tile_diagonally_scaled_matrix_commutator_s12_kernel(
         VC = nc.vector.tensor_copy
         permute_u_scales()
         permute_u(0)
-        turn_x(0)
         products("a00")
         group_w(0)
-        quantize("x0")
-        quantize("w0")
+        turn_x(0)
         products("a01")
+        quantize("w0")
+        quantize("x0")
         weave("a00")
         widen_left()
         permute_u(1)
@@ -345,12 +362,12 @@ def tile_diagonally_scaled_matrix_commutator_s12_kernel(
         quantize("ta01")
         quantize("sa10")
         turn("a10")
-        products("b10", terms(0, 0, 0))
+        products("b10", terms(0, 0, 0)[:3])
         weave("b01")
         quantize("ta10")
         quantize("sb01")
         turn("b01")
-        products("a11")
+        products("a11", terms(0, 0, 0)[3:])
         weave("b10")
         quantize("tb01")
         quantize("sb10")
@@ -364,9 +381,9 @@ def tile_diagonally_scaled_matrix_commutator_s12_kernel(
         finish(0, 0, 3)
         quantize("tb10")
         turn("a11")
+        turn("b11")
         weave("b11")
         run(terms(0, 1, 2))
-        turn("b11")
         quantize("ta11")
         quantize("sb11")
         run(terms(0, 1, 0) + terms(0, 1, 3))

@@ -17,7 +17,7 @@ MULT = mybir.AluOpType.mult
 
 P = 128
 H = 512
-WARM = 24
+WARM = 21
 
 
 def tile_diagonally_scaled_matrix_commutator_s12_kernel(
@@ -55,12 +55,14 @@ def tile_diagonally_scaled_matrix_commutator_s12_kernel(
         warm_codes = kept("warm_codes", P, U32)
         warm_scales = kept("warm_scales", P, U8)
         nc.vector.memset(warm_in[:], 0.0)
-        u_plane = kept("u_plane", 2 * N, U8)
-        v_plane = kept("v_plane", 2 * N, U8)
-        u_sc = kept("u_sc", 2 * N, U8)
-        nc.vector.memset(v_plane[:].bitcast(I32), 0)
+        u_plane = [kept("u_plane0", 2 * H, U8), kept("u_plane1", 2 * H, U8)]
+        v_plane = [kept("v_plane0", 2 * H, U8), kept("v_plane1", 2 * H, U8)]
+        u_sc = [kept("u_sc0", 2 * H, U8), kept("u_sc1", 2 * H, U8)]
+        nc.vector.memset(v_plane[0][:].bitcast(I32), 0)
         nc.vector.quantize_mx(out=warm_codes[:].bitcast(FP8X4), scales=warm_scales[:], in_=warm_in[:])
-        nc.vector.memset(u_sc[:].bitcast(I32), 0)
+        nc.vector.memset(u_sc[0][:].bitcast(I32), 0)
+        nc.vector.memset(v_plane[1][:].bitcast(I32), 0)
+        nc.vector.memset(u_plane[1][:].bitcast(I32), 0)
         warm_bank = bank_tile("warm_bank", 7)
         for rep in range(WARM):
             nc.tensor.matmul_mx(
@@ -81,11 +83,11 @@ def tile_diagonally_scaled_matrix_commutator_s12_kernel(
                 in_=words.bitcast(I32)[:, :, h * 256 : (h + 1) * 256].rearrange("g p c -> p g c"),
             )
 
-        def load_plane(plane, scales, queues):
+        def load_plane(plane, scales, h):
             for quad in range(4):
-                queues[quad].dma_start(
-                    out=plane[32 * quad : 32 * quad + 4, :].bitcast(I32).rearrange("r (g c) -> r g c", g=2),
-                    in_=scales.bitcast(I32)[:, 4 * quad : 4 * quad + 4, :].rearrange("g r c -> r g c"),
+                nc.sync.dma_start(
+                    out=plane[h][32 * quad : 32 * quad + 4, :].bitcast(I32).rearrange("r (g c) -> r g c", g=2),
+                    in_=scales.bitcast(I32)[:, 4 * quad : 4 * quad + 4, h * P : (h + 1) * P].rearrange("g r c -> r g c"),
                 )
 
         def load_x(h):
@@ -102,28 +104,29 @@ def tile_diagonally_scaled_matrix_commutator_s12_kernel(
                 in_=w[:, g * H : (g + 1) * H].rearrange("(p j) n -> p j n", j=4),
             )
 
-        load_plane(u_plane, u_scales, [nc.sync] * 4)
+        load_plane(u_plane, u_scales, 0)
         load_words(u_raw, "u_raw", u_words, 0)
         load_words(v_codes, "v_codes", v_words, 0)
-        load_plane(v_plane, v_scales, [nc.sync] * 4)
+        load_plane(v_plane, v_scales, 0)
         load_x(0)
         load_w(0)
+        load_plane(v_plane, v_scales, 1)
         load_words(v_codes, "v_codes", v_words, 1)
         nc.sync.dma_start(out=left_rows[0:8, :], in_=left.rearrange("(c p) -> c p", p=P))
-        load_words(u_raw, "u_raw", u_words, 1)
         load_x(1)
+        load_plane(u_plane, u_scales, 1)
+        load_words(u_raw, "u_raw", u_words, 1)
         load_w(1)
         right_all = kept("right_all", N, BF16)
         nc.sync.dma_start(out=right_all[:], in_=right.partition_broadcast(P))
 
         u_codes = {}
 
-        def permute_u_scales():
-            for quad in range(4):
-                rows = slice(32 * quad, 32 * quad + 4)
+        def permute_u_scales(g, row_sets):
+            for rows in row_sets:
                 nc.vector.tensor_copy(
-                    out=u_sc[rows, :].bitcast(I32).rearrange("p (s t q c) -> p s t q c", s=4, t=4, q=16),
-                    in_=u_plane[rows, :].bitcast(I32).rearrange("p (s q t c) -> p s t q c", s=4, t=4, q=16),
+                    out=u_sc[g][rows, :].bitcast(I32).rearrange("p (s t q c) -> p s t q c", s=2, t=4, q=16),
+                    in_=u_plane[g][rows, :].bitcast(I32).rearrange("p (s q t c) -> p s t q c", s=2, t=4, q=16),
                 )
 
         def permute_u(g):
@@ -180,9 +183,9 @@ def tile_diagonally_scaled_matrix_commutator_s12_kernel(
                     nc.tensor.matmul_mx(
                         out=bank[:],
                         lhsT=u_codes[g][:, s * 1024 + t * 256 : s * 1024 + (t + 1) * 256].bitcast(FP4X4),
-                        lhsT_scale=u_sc[:, s * N + g * H + t * P : s * N + g * H + (t + 1) * P],
+                        lhsT_scale=u_sc[g][:, s * H + t * P : s * H + (t + 1) * P],
                         rhs=v_codes[h][:, s * 1024 : (s + 1) * 1024].bitcast(FP4X4),
-                        rhs_scale=v_plane[:, s * N + h * H : s * N + (h + 1) * H],
+                        rhs_scale=v_plane[h][:, s * H : (s + 1) * H],
                         start=(s == 0),
                         stop=(s == 1),
                     )
@@ -284,6 +287,19 @@ def tile_diagonally_scaled_matrix_commutator_s12_kernel(
                 )
             nc.sync.dma_start(out=out[i * P : (i + 1) * P, b * H : (b + 1) * H], in_=res[:])
 
+        def finish_split(a, b, c):
+            key = (a, b, c)
+            i = 4 * a + c
+            half_done = work.tile([P, H], F32, name="half_done%d%d%d" % key, tag="half_done", bufs=3)
+            nc.scalar.activation(
+                out=half_done[:].rearrange("p (q u s) -> p q u s", q=16, u=2),
+                in_=acc[key][:].rearrange("p (u q s) -> p q u s", q=16, u=2),
+                func=mybir.ActivationFunctionType.Copy, scale=left_cols[:, i : i + 1],
+            )
+            res = work.tile([P, H], F32, name="res%d%d%d" % key, tag="res", bufs=6)
+            nc.vector.tensor_tensor(out=res[:], in0=half_done[:], in1=right_all[:, b * H : (b + 1) * H], op=MULT)
+            nc.sync.dma_start(out=out[i * P : (i + 1) * P, b * H : (b + 1) * H], in_=res[:])
+
         def last_tile(a, b, c):
             i = 4 * a + c
             for half in range(2):
@@ -328,49 +344,50 @@ def tile_diagonally_scaled_matrix_commutator_s12_kernel(
             return [(a, b, c, term) for c in range(4)]
 
         VC = nc.vector.tensor_copy
-        permute_u_scales()
+        permute_u_scales(0, [slice(32 * quad, 32 * quad + 4) for quad in range(4)])
         permute_u(0)
         products("a00")
         group_w(0)
         turn_x(0)
+        turn("a00")
         products("a01")
         quantize("w0")
         quantize("x0")
         weave("a00")
         widen_left()
         permute_u(1)
+        permute_u_scales(1, [slice(0, P)])
         products("b00")
         quantize("sa00")
-        weave("a01")
-        turn("a00")
+        group_w(1)
         turn_x(1, copy=VC)
         turn_left()
         weave("b00")
         quantize("x1")
         quantize("sb00")
         products("a10")
+        quantize("w1")
         quantize("ta00")
-        group_w(1)
         narrow_ring()
         turn("b00")
         turn("a01")
-        quantize("sa01")
-        quantize("w1")
         quantize("tb00")
-        products("b01", terms(0, 0, 2))
         weave("a10")
-        quantize("ta01")
+        products("b01", [None] + terms(0, 0, 2)[:3])
+        run(terms(0, 0, 2)[3:])
         quantize("sa10")
-        turn("a10")
-        products("b10", terms(0, 0, 0)[:3])
-        weave("b01")
-        quantize("ta10")
-        quantize("sb01")
+        quantize("ta01")
+        weave("a01")
+        products("b10", terms(0, 0, 0))
         turn("b01")
-        products("a11", terms(0, 0, 0)[3:])
+        weave("b01")
+        quantize("sa01")
         weave("b10")
         quantize("tb01")
         quantize("sb10")
+        products("a11")
+        quantize("sb01")
+        turn("a10")
         turn("b10")
         products("b11", terms(0, 0, 1) + terms(0, 0, 3))
         weave("a11")
@@ -380,6 +397,7 @@ def tile_diagonally_scaled_matrix_commutator_s12_kernel(
         finish(0, 0, 2)
         finish(0, 0, 3)
         quantize("tb10")
+        quantize("ta10")
         turn("a11")
         turn("b11")
         weave("b11")
@@ -391,11 +409,11 @@ def tile_diagonally_scaled_matrix_commutator_s12_kernel(
         for c in range(4):
             for term in (0, 2, 1, 3):
                 accumulate(1, 0, c, term, stage_bank)
-            finish(1, 0, c)
+            finish_split(1, 0, c)
             accumulate(0, 1, c, 1)
             finish(0, 1, c)
         for c in range(3):
             for term in range(4):
                 accumulate(1, 1, c, term)
-            finish(1, 1, c)
+            (finish_split if c % 2 == 0 and c < 2 else finish)(1, 1, c)
         last_tile(1, 1, 3)

from contextlib import ExitStack

import concourse.mybir as mybir
from concourse.masks import make_identity

N, K, L = 1024, 1024, 512
FLOPS = 2 * N * N * K + 2 * N * N * L + 4 * N * N * N

F32 = mybir.dt.float32
BF16 = mybir.dt.bfloat16
I32 = mybir.dt.int32
U32 = mybir.dt.uint32
U8 = mybir.dt.uint8
FP8X4 = mybir.dt.float8_e4m3fn_x4
FP4X4 = mybir.dt.float4_e2m1fn_x4
MULT = mybir.AluOpType.mult

P = 128
H = 512
WARM = 21


def tile_diagonally_scaled_matrix_commutator_s12_kernel(
    tc, u_words, u_scales, v_words, v_scales, x, w, left, right, out
):
    nc = tc.nc
    with ExitStack() as ctx:
        keep = ctx.enter_context(tc.tile_pool(name="keep", bufs=1))
        work = ctx.enter_context(tc.tile_pool(name="work", bufs=3))
        psum = ctx.enter_context(tc.psum_pool(name="psum", bufs=1))
        ctx.enter_context(tc.manual_schedule())

        def kept(name, width, dtype):
            return keep.tile([P, width], dtype, name=name, align_bytes=64)

        ring = {"banks": list(range(8)), "next": 0, "acc": 4}

        def bank_tile(name, b):
            return psum.tile([P, H], F32, name=name, tag="bank%d" % b)

        def stage_bank(name):
            b = ring["banks"][ring["next"] % len(ring["banks"])]
            ring["next"] = ring["next"] + 1
            return bank_tile(name, b)

        def narrow_ring():
            ring["banks"] = list(range(4))

        def acc_bank(name):
            b = ring["acc"]
            ring["acc"] = 4 + (b + 1) % 4
            return bank_tile(name, b)

        warm_in = kept("warm_in", 4 * P, BF16)
        warm_codes = kept("warm_codes", P, U32)
        warm_scales = kept("warm_scales", P, U8)
        nc.vector.memset(warm_in[:], 0.0)
        u_plane = [kept("u_plane0", 2 * H, U8), kept("u_plane1", 2 * H, U8)]
        v_plane = [kept("v_plane0", 2 * H, U8), kept("v_plane1", 2 * H, U8)]
        u_sc = [kept("u_sc0", 2 * H, U8), kept("u_sc1", 2 * H, U8)]
        nc.vector.memset(v_plane[0][:].bitcast(I32), 0)
        nc.vector.quantize_mx(out=warm_codes[:].bitcast(FP8X4), scales=warm_scales[:], in_=warm_in[:])
        nc.vector.memset(u_sc[0][:].bitcast(I32), 0)
        nc.vector.memset(v_plane[1][:].bitcast(I32), 0)
        nc.vector.memset(u_plane[1][:].bitcast(I32), 0)
        warm_bank = bank_tile("warm_bank", 7)
        for rep in range(WARM):
            nc.tensor.matmul_mx(
                out=warm_bank[:, 0:P], lhsT=warm_codes[:].bitcast(FP8X4), lhsT_scale=warm_scales[:],
                rhs=warm_codes[:].bitcast(FP8X4), rhs_scale=warm_scales[:], start=True, stop=True,
            )
        ident = kept("ident", P, F32)
        make_identity(nc, ident[:])
        left_rows = kept("left_rows", P, BF16)
        nc.gpsimd.memset(left_rows[:], 0.0)

        u_raw, v_codes, x_raw, w_raw = {}, {}, {}, {}

        def load_words(store, name, words, h):
            store[h] = kept("%s%d" % (name, h), 4 * H, U8)
            nc.sync.dma_start(
                out=store[h][:].bitcast(I32).rearrange("p (g c) -> p g c", g=2),
                in_=words.bitcast(I32)[:, :, h * 256 : (h + 1) * 256].rearrange("g p c -> p g c"),
            )

        def load_plane(plane, scales, h):
            for quad in range(4):
                nc.sync.dma_start(
                    out=plane[h][32 * quad : 32 * quad + 4, :].bitcast(I32).rearrange("r (g c) -> r g c", g=2),
                    in_=scales.bitcast(I32)[:, 4 * quad : 4 * quad + 4, h * P : (h + 1) * P].rearrange("g r c -> r g c"),
                )

        def load_x(h):
            x_raw[h] = kept("x_raw%d" % h, 4 * L, BF16)
            nc.sync.dma_start(
                out=x_raw[h][:].rearrange("p (c k) -> p c k", c=4),
                in_=x[h * H : (h + 1) * H, :].rearrange("(c p) k -> p c k", p=P),
            )

        def load_w(g):
            w_raw[g] = kept("w_raw%d" % g, 4 * H, BF16)
            nc.sync.dma_start(
                out=w_raw[g][:].rearrange("p (j n) -> p j n", j=4),
                in_=w[:, g * H : (g + 1) * H].rearrange("(p j) n -> p j n", j=4),
            )

        load_plane(u_plane, u_scales, 0)
        load_words(u_raw, "u_raw", u_words, 0)
        load_words(v_codes, "v_codes", v_words, 0)
        load_plane(v_plane, v_scales, 0)
        load_x(0)
        load_w(0)
        load_plane(v_plane, v_scales, 1)
        load_words(v_codes, "v_codes", v_words, 1)
        nc.sync.dma_start(out=left_rows[0:8, :], in_=left.rearrange("(c p) -> c p", p=P))
        load_x(1)
        load_plane(u_plane, u_scales, 1)
        load_words(u_raw, "u_raw", u_words, 1)
        load_w(1)
        right_all = kept("right_all", N, BF16)
        nc.sync.dma_start(out=right_all[:], in_=right.partition_broadcast(P))

        u_codes = {}

        def permute_u_scales(g, row_sets):
            for rows in row_sets:
                nc.vector.tensor_copy(
                    out=u_sc[g][rows, :].bitcast(I32).rearrange("p (s t q c) -> p s t q c", s=2, t=4, q=16),
                    in_=u_plane[g][rows, :].bitcast(I32).rearrange("p (s q t c) -> p s t q c", s=2, t=4, q=16),
                )

        def permute_u(g):
            u_codes[g] = kept("u_codes%d" % g, 4 * H, U8)
            nc.vector.tensor_copy(
                out=u_codes[g][:].bitcast(I32).rearrange("p (s t q c) -> p s t q c", s=2, t=4, q=16),
                in_=u_raw[g][:].bitcast(I32).rearrange("p (s q t c) -> p s t q c", s=2, t=4, q=16),
            )

        grouped, quant = {}, {}

        def new_grouped(key):
            grouped[key] = work.tile([P, 4 * H], BF16, name="grouped_%s" % (key,), tag="grouped", bufs=8, align_bytes=64)
            return grouped[key]

        def quantize(key):
            codes = kept("codes_%s" % (key,), H, U32)
            scales = kept("scales_%s" % (key,), H, U8)
            nc.vector.quantize_mx(out=codes[:].bitcast(FP8X4), scales=scales[:], in_=grouped[key][:])
            quant[key] = (codes, scales)

        def turn_x(h, new_bank=stage_bank, copy=nc.scalar.copy):
            dst = new_grouped("x%d" % h)[:].bitcast(F32).rearrange("p (u a q s e) -> p a u q s e", u=2, a=2, q=8, e=2)
            words = x_raw[h][:].bitcast(F32)
            banks = []
            for a in range(2):
                bank = new_bank("xt%d%d" % (h, a))
                banks.append(bank)
                for e in range(2):
                    for c in range(2):
                        c0 = (2 * a + c) * 256
                        nc.tensor.transpose(bank[:, (2 * e + c) * P : (2 * e + c + 1) * P], words[:, c0 + e : c0 + 256 : 2], ident[:])
            for a in range(2):
                copy(out=dst[:, a], in_=banks[a][:].rearrange("p (e q u s) -> p u q s e", e=2, q=8, u=2))

        def group_w(g):
            dst = new_grouped("w%d" % g)
            for c in range(2):
                nc.vector.tensor_copy(
                    out=dst[:].rearrange("p (t q c i j) -> p c t q j i", t=4, q=16, i=4, j=4)[:, c],
                    in_=w_raw[g][:].rearrange("p (j q t c i) -> p c t q j i", j=4, q=16, t=4, i=4)[:, c],
                )

        plain = {}

        def product(kind, g, h, t):
            key = "%s%d%d" % (kind, g, h)
            if t == 0:
                plain[key] = work.tile([P, 4 * H], BF16, name="plain_" + key, tag="plain", bufs=6, align_bytes=64)
            bank = stage_bank("mm_%s%d" % (key, t))
            dst = plain[key][:, t * H : (t + 1) * H]
            if kind == "a":
                for s in range(2):
                    nc.tensor.matmul_mx(
                        out=bank[:],
                        lhsT=u_codes[g][:, s * 1024 + t * 256 : s * 1024 + (t + 1) * 256].bitcast(FP4X4),
                        lhsT_scale=u_sc[g][:, s * H + t * P : s * H + (t + 1) * P],
                        rhs=v_codes[h][:, s * 1024 : (s + 1) * 1024].bitcast(FP4X4),
                        rhs_scale=v_plane[h][:, s * H : (s + 1) * H],
                        start=(s == 0),
                        stop=(s == 1),
                    )
                nc.scalar.copy(
                    out=dst.rearrange("p (u q s) -> p u q s", u=2, q=16),
                    in_=bank[:].rearrange("p (q u s) -> p u q s", u=2, q=16),
                )
            else:
                wc, ws = quant["w%d" % g]
                xc, xs = quant["x%d" % h]
                nc.tensor.matmul_mx(
                    out=bank[:],
                    lhsT=wc[:, t * P : (t + 1) * P].bitcast(FP8X4),
                    lhsT_scale=ws[:, t * P : (t + 1) * P],
                    rhs=xc[:].bitcast(FP8X4),
                    rhs_scale=xs[:],
                    start=True,
                    stop=True,
                )
                nc.scalar.copy(out=dst, in_=bank[:])

        def weave(key):
            dst = new_grouped("s" + key)
            if key[0] == "a":
                nc.vector.tensor_scalar(
                    out=dst[:].rearrange("p (c i t) -> p c t i", i=4, t=4),
                    in0=plain[key][:].rearrange("p (t c i) -> p c t i", i=4, t=4),
                    scalar1=-1.0, scalar2=None, op0=MULT,
                )
            else:
                for u in range(2):
                    nc.vector.tensor_copy(
                        out=dst[:].rearrange("p (q u c i t) -> p u q c t i", q=16, u=2, i=4, t=4)[:, u],
                        in_=plain[key][:].rearrange("p (t u q c i) -> p u q c t i", q=16, u=2, i=4, t=4)[:, u],
                    )

        def turn(key, new_bank=stage_bank, copy=(nc.scalar.copy, nc.scalar.copy)):
            dst = new_grouped("t" + key)[:].bitcast(F32).rearrange(
                "p (q a t r u) -> p a q t r u" if key[0] == "a" else "p (a q t r u) -> p a q t r u", q=16, a=2, t=2, u=2
            )
            words = plain[key][:].bitcast(F32)
            banks = []
            for a in range(2):
                bank = new_bank("tr_%s%d" % (key, a))
                banks.append(bank)
                for j in range(4):
                    nc.tensor.transpose(bank[:, j * P : (j + 1) * P], words[:, (4 * a + j) * P : (4 * a + j + 1) * P], ident[:])
            for a in range(2):
                copy[a](out=dst[:, a], in_=banks[a][:].rearrange("p (t u q r) -> p q t r u", t=2, u=2, q=16))

        left_cols = kept("left_cols", 8, F32)

        rows32 = kept("left_rows32", P, F32)

        def widen_left():
            nc.vector.tensor_copy(out=rows32[:], in_=left_rows[:])

        def turn_left():
            bank = stage_bank("left_bank")
            nc.tensor.transpose(bank[:, 0:P], rows32[:], ident[:])
            nc.scalar.copy(out=left_cols[:], in_=bank[:, 0:8])

        def operands(a, b, term):
            k = term % 2
            if term < 2:
                return quant["ta%d%d" % (a, k)], quant["tb%d%d" % (b, k)]
            return quant["sb%d%d" % (k, a)], quant["sa%d%d" % (k, b)]

        acc, done = {}, {}

        def accumulate(a, b, c, term, new_bank=acc_bank):
            key = (a, b, c)
            if key not in acc:
                acc[key] = new_bank("acc%d%d%d" % key)
                done[key] = 0
            (lc, ls), (rc, rs) = operands(a, b, term)
            nc.tensor.matmul_mx(
                out=acc[key][:],
                lhsT=lc[:, c * P : (c + 1) * P].bitcast(FP8X4),
                lhsT_scale=ls[:, c * P : (c + 1) * P],
                rhs=rc[:].bitcast(FP8X4),
                rhs_scale=rs[:],
                start=(done[key] == 0),
                stop=(done[key] == 3),
            )
            done[key] = done[key] + 1

        def finish(a, b, c):
            key = (a, b, c)
            res = work.tile([P, H], F32, name="res%d%d%d" % key, tag="res", bufs=6)
            i = 4 * a + c
            for u in range(2):
                nc.vector.scalar_tensor_tensor(
                    out=res[:].rearrange("p (q u s) -> p u q s", q=16, u=2)[:, u],
                    in0=acc[key][:, u * 256 : (u + 1) * 256].rearrange("p (q s) -> p q s", q=16),
                    scalar=left_cols[:, i : i + 1],
                    in1=right_all[:, b * H : (b + 1) * H].rearrange("p (q u s) -> p u q s", q=16, u=2)[:, u],
                    op0=MULT, op1=MULT,
                )
            nc.sync.dma_start(out=out[i * P : (i + 1) * P, b * H : (b + 1) * H], in_=res[:])

        def finish_split(a, b, c):
            key = (a, b, c)
            i = 4 * a + c
            half_done = work.tile([P, H], F32, name="half_done%d%d%d" % key, tag="half_done", bufs=3)
            nc.scalar.activation(
                out=half_done[:].rearrange("p (q u s) -> p q u s", q=16, u=2),
                in_=acc[key][:].rearrange("p (u q s) -> p q u s", q=16, u=2),
                func=mybir.ActivationFunctionType.Copy, scale=left_cols[:, i : i + 1],
            )
            res = work.tile([P, H], F32, name="res%d%d%d" % key, tag="res", bufs=6)
            nc.vector.tensor_tensor(out=res[:], in0=half_done[:], in1=right_all[:, b * H : (b + 1) * H], op=MULT)
            nc.sync.dma_start(out=out[i * P : (i + 1) * P, b * H : (b + 1) * H], in_=res[:])

        def last_tile(a, b, c):
            i = 4 * a + c
            for half in range(2):
                res = work.tile([P, 256], F32, name="last_res%d" % half, tag="res", bufs=6)
                out_cols = slice(b * H + half * 256, b * H + (half + 1) * 256)
                for u in range(2):
                    cols = slice(u * 256 + half * P, u * 256 + (half + 1) * P)
                    bank = stage_bank("last%d%d" % (half, u))
                    for term in range(4):
                        (lc, ls), (rc, rs) = operands(a, b, term)
                        nc.tensor.matmul_mx(
                            out=bank[:, 0:P],
                            lhsT=lc[:, c * P : (c + 1) * P].bitcast(FP8X4),
                            lhsT_scale=ls[:, c * P : (c + 1) * P],
                            rhs=rc[:, cols].bitcast(FP8X4),
                            rhs_scale=rs[:, cols],
                            start=(term == 0),
                            stop=(term == 3),
                        )
                    nc.vector.scalar_tensor_tensor(
                        out=res[:].rearrange("p (q u s) -> p u q s", q=8, u=2)[:, u],
                        in0=bank[:, 0:P].rearrange("p (q s) -> p q s", q=8),
                        scalar=left_cols[:, i : i + 1],
                        in1=right_all[:, out_cols].rearrange("p (q u s) -> p u q s", q=8, u=2)[:, u],
                        op0=MULT, op1=MULT,
                    )
                nc.sync.dma_start(out=out[i * P : (i + 1) * P, out_cols], in_=res[:])

        def run(jobs):
            for job in jobs:
                accumulate(*job)

        def products(key, fill=(), slots=range(4)):
            fill = list(fill)
            for t in slots:
                for job in fill[t::4]:
                    if job:
                        accumulate(*job)
                product(key[0], int(key[1]), int(key[2]), t)

        def terms(a, b, term):
            return [(a, b, c, term) for c in range(4)]

        VC = nc.vector.tensor_copy
        permute_u_scales(0, [slice(32 * quad, 32 * quad + 4) for quad in range(4)])
        permute_u(0)
        products("a00")
        group_w(0)
        turn_x(0)
        turn("a00")
        products("a01")
        quantize("w0")
        quantize("x0")
        weave("a00")
        widen_left()
        permute_u(1)
        permute_u_scales(1, [slice(0, P)])
        products("b00")
        quantize("sa00")
        group_w(1)
        turn_x(1, copy=VC)
        turn_left()
        weave("b00")
        quantize("x1")
        quantize("sb00")
        products("a10")
        quantize("w1")
        quantize("ta00")
        narrow_ring()
        turn("b00")
        turn("a01")
        quantize("tb00")
        weave("a10")
        products("b01", [None] + terms(0, 0, 2)[:3])
        run(terms(0, 0, 2)[3:])
        quantize("sa10")
        quantize("ta01")
        weave("a01")
        products("b10", terms(0, 0, 0))
        turn("b01")
        weave("b01")
        quantize("sa01")
        weave("b10")
        quantize("tb01")
        quantize("sb10")
        products("a11")
        quantize("sb01")
        turn("a10")
        turn("b10")
        products("b11", terms(0, 0, 1) + terms(0, 0, 3))
        weave("a11")
        finish(0, 0, 0)
        finish(0, 0, 1)
        quantize("sa11")
        finish(0, 0, 2)
        finish(0, 0, 3)
        quantize("tb10")
        quantize("ta10")
        turn("a11")
        turn("b11")
        weave("b11")
        run(terms(0, 1, 2))
        quantize("ta11")
        quantize("sb11")
        run(terms(0, 1, 0) + terms(0, 1, 3))
        quantize("tb11")
        for c in range(4):
            for term in (0, 2, 1, 3):
                accumulate(1, 0, c, term, stage_bank)
            finish_split(1, 0, c)
            accumulate(0, 1, c, 1)
            finish(0, 1, c)
        for c in range(3):
            for term in range(4):
                accumulate(1, 1, c, term)
            (finish_split if c % 2 == 0 and c < 2 else finish)(1, 1, c)
        last_tile(1, 1, 3)
